import numpy as np
import ml_dtypes


def mxq(x, axis, fmt="e4m3"):
    dtype, down = {"e4m3": (ml_dtypes.float8_e4m3fn, 7), "e5m2": (ml_dtypes.float8_e5m2, 14)}[fmt]
    v = np.moveaxis(np.asarray(x, np.float32).astype(ml_dtypes.bfloat16).astype(np.float64), axis, -1)
    blocks = v.reshape(v.shape[:-1] + (-1, 32))
    amax = np.abs(blocks).max(-1, keepdims=True)
    byte = np.maximum(np.where(amax > 0, np.frexp(amax)[1] - 1 + 127, 0) - down, 1)
    scale = np.exp2(byte - 127.0)
    codes = (blocks / scale).astype(np.float32).astype(dtype).astype(np.float64)
    return np.moveaxis((codes * scale).reshape(v.shape), -1, axis)


WIDE = False


def mx_kscale(k):
    if not WIDE:
        return np.ones(k)
    levels = np.array([10, -10, 5, -5, 0])
    if k % 512:
        return np.exp2(np.random.permutation(np.resize(levels, k // 32))).repeat(32)
    a = np.empty((k // 512, 16))
    for p in range(k // 512):
        a[p, :8] = np.random.permutation(np.resize(levels, 8))
        for g in range(8):
            far = levels[np.abs(levels - a[p, g]) >= 10]
            a[p, g + 8] = far[np.random.randint(len(far))]
    return np.exp2(a.ravel()).repeat(32)


def f64(x):
    return np.asarray(x).astype(np.float64)


def striped(idx):
    return np.tile(idx.reshape(-1, 16).T, (8, 1)).astype(np.uint16)


def unstriped(offs):
    return offs[:16].T.reshape(-1).astype(np.int64)


def striped8(idx):
    return np.concatenate([x.reshape(-1, 16).T for x in idx]).astype(np.uint16)


def runs(offs, k):
    lists = np.stack([offs[16 * r : 16 * r + 16].T.reshape(-1) for r in range(8)]).astype(np.int64)
    return lists[np.arange(k) % 512 // 64]


def pack_weight(w):
    k, n = w.shape
    w = f64(np.asarray(w, np.float32).astype(ml_dtypes.bfloat16)).reshape(k // 32, 32, n)
    amax = np.abs(w).max(1)
    byte = np.clip(np.where(amax > 0, np.frexp(amax)[1] - 1 + 127 - 7, 1), 1, 254)
    scaled = (w * np.exp2(127.0 - byte)[:, None, :]).reshape(k, n).astype(np.float32)
    words = np.ascontiguousarray(scaled.reshape(k // 512, 128, 4, n).transpose(0, 1, 3, 2)).astype(ml_dtypes.float8_e4m3fn).view(np.uint8)
    return words, np.ascontiguousarray(byte.astype(np.uint8).reshape(k // 512, 16, n))


def unpack_weight(words, scales):
    g, p, n, _ = words.shape
    vals = np.ascontiguousarray(words).view(ml_dtypes.float8_e4m3fn).astype(np.float64) * np.repeat(np.exp2(scales.astype(np.float64) - 127.0), 8, axis=1)[..., None]
    return vals.transpose(0, 1, 3, 2).reshape(g * 512, n)


K, T, S, N, G, H = 512, 2048, 512, 512, 2048, 512


def setup_inputs():
    n = np.random.standard_normal
    s = mx_kscale(K)[:, None]
    u = mx_kscale(S)
    packed_xT = pack_weight(n((K, T)) * s)
    packed_dT = pack_weight(n((K, G)) / s)
    return {
        "x_words": packed_xT[0],
        "x_scales": packed_xT[1],
        "d_words": packed_dT[0],
        "d_scales": packed_dT[1],
        "gn": (np.random.uniform(0.5, 1.5, (H, 1)) * u[:, None]).astype(np.float32),
        "w1": (n((H, N)) / np.sqrt(H) / u[:, None]).astype(np.float32),
        "offs": striped(np.random.permutation(T)[:S]),
        "kidx": striped8(np.random.randint(0, G, (8, H))),
        "n1": striped8(np.stack([np.random.permutation(S) for _ in range(8)])),
        "n2": striped8(np.stack([np.random.permutation(S) for _ in range(8)])),
        "n3": striped8(np.stack([np.random.permutation(S) for _ in range(8)])),
        "n4": striped8(np.stack([np.random.permutation(S) for _ in range(8)])),
        "n5": striped8(np.stack([np.random.permutation(S) for _ in range(8)])),
    }


def reference(x_words, x_scales, d_words, d_scales, gn, w1, offs, kidx, n1, n2, n3, n4, n5):
    d_kidx = unpack_weight(d_words, d_scales)[np.arange(K)[:, None], runs(kidx, K)]
    xq = unpack_weight(x_words, x_scales)[:, unstriped(offs)]
    s = 0.0625 * (d_kidx.T @ xq)
    z = f64(gn) * (s + s[np.arange(H)[:, None], runs(n1, H)] - (np.maximum(s[np.arange(H)[:, None], runs(n2, H)], s[np.arange(H)[:, None], runs(n3, H)])))
    h = mxq(f64(w1), 0, "e4m3").T @ mxq(z, 0, "e4m3")
    return (h[np.arange(N)[:, None], runs(n4, N)]) / (np.abs(h) + np.abs(h[np.arange(N)[:, None], runs(n5, N)]) + 0.5)

@@ -1,0 +1,198 @@
+from contextlib import ExitStack
+
+import concourse.mybir as mybir
+
+K, T, S, N, G, H = 512, 2048, 512, 512, 2048, 512
+FLOPS = 2 * K * H * S + 2 * H * N * S
+
+F32 = mybir.dt.float32
+BF16 = mybir.dt.bfloat16
+I32 = mybir.dt.int32
+U32 = mybir.dt.uint32
+U16 = mybir.dt.uint16
+U8 = mybir.dt.uint8
+FP8X4 = mybir.dt.float8_e4m3fn_x4
+ALU = mybir.AluOpType
+ACT = mybir.ActivationFunctionType
+
+P = 128
+PACK = 4
+STRIPE = 16
+
+
+def tile_picked_keytrimnorm2_none_p_kernel(tc, x_words, x_scales, d_words, d_scales, gn, w1, offs, kidx, n1, n2, n3, n4, n5, out):
+    nc = tc.nc
+    with ExitStack() as ctx:
+        keep = ctx.enter_context(tc.tile_pool(name="keep", bufs=1))
+        psum = ctx.enter_context(tc.psum_pool(name="psum", bufs=1))
+
+        def load_list(src, name):
+            t = keep.tile([P, S // STRIPE], U16, name=name)
+            nc.sync.dma_start(t[:], src)
+            return t
+
+        def entries(lst, a, b):
+            return lst[:, a // STRIPE : b // STRIPE]
+
+        d_byte_table = keep.tile([P, G], U8, name="d_byte_table")
+        x_byte_table = keep.tile([P, T], U8, name="x_byte_table")
+        d_plane = keep.tile([P, H], U8, name="d_plane", align_bytes=64)
+        nc.gpsimd.memset(d_byte_table[:].bitcast(I32), 0)
+        nc.vector.memset(x_byte_table[:].bitcast(I32), 0)
+        nc.gpsimd.memset(d_plane[:].bitcast(I32), 0)
+
+        kidx_t = load_list(kidx, "kidx_t")
+        nc.scalar.dma_start(d_byte_table[0:P:8, :].bitcast(I32), d_scales[0].bitcast(I32))
+        d_word_table = keep.tile([P, G], U32, name="d_word_table")
+        nc.sync.dma_start(d_word_table[:].bitcast(I32), d_words[0].rearrange("p c r -> p (c r)").bitcast(I32))
+        offs_t = load_list(offs, "offs_t")
+        x_word_table = keep.tile([P, T], U32, name="x_word_table", tag="big")
+        nc.sync.dma_start(x_word_table[:].bitcast(I32), x_words[0].rearrange("p c r -> p (c r)").bitcast(I32))
+        for q in range(4):
+            nc.scalar.dma_start(x_byte_table[32 * q : 32 * q + 4, :].bitcast(I32), x_scales[0, 4 * q : 4 * q + 4, :].bitcast(I32))
+        n1_t = load_list(n1, "n1_t")
+        n2_t = load_list(n2, "n2_t")
+        n3_t = load_list(n3, "n3_t")
+        gn_t = keep.tile([P, PACK], F32, name="gn_t")
+        nc.sync.dma_start(gn_t[:], gn.rearrange("(p t) o -> p (t o)", t=PACK))
+        n5_t = load_list(n5, "n5_t")
+        n4_t = load_list(n4, "n4_t")
+
+        warm = keep.tile([P, 1], F32, name="warm")
+        nc.scalar.activation(warm[:], gn_t[:, 0:1], ACT.Abs_reciprocal_sqrt, scale=0.0, bias=1.0)
+
+        last = PACK - 1
+        s_win = [keep.tile([P, S if t in (0, last) else 2 * S], F32, name=f"s_win{t}") for t in range(PACK)]
+        h_win = [keep.tile([P, 2 * S], F32, name=f"h_win{t}") for t in range(PACK)]
+        a_win = [keep.tile([P, 2 * S], F32, name=f"a_win{t}") for t in range(PACK)]
+        s_own = [s_win[t + 1][:, S:] for t in range(last - 1)]
+        s_own.extend(keep.tile([P, S], F32, name=f"s_own{t}")[:] for t in (last - 1, last))
+        e = [a_win[t][:, S:] for t in range(PACK)]
+        u = [h_win[t][:, S:] for t in range(PACK)]
+
+        d_bytes = keep.tile([P, H], U8, name="d_bytes", tag="picked")
+        nc.vector.tensor_copy(d_bytes[:], d_byte_table[:].indirect(kidx_t[:]))
+        d_bytes_dealt = keep.tile([P, H], U8, name="d_bytes_dealt")
+        nc.vector.tensor_copy(d_bytes_dealt[:].rearrange("p (t m) -> p t m", t=PACK), d_bytes[:].rearrange("p (m t) -> p t m", t=PACK))
+        for r in range(4):
+            nc.sync.dma_start(d_plane[r:P:32, :].bitcast(I32), d_bytes_dealt[8 * r : P : 32, :].bitcast(I32))
+        x_plane = keep.tile([P, S], U8, name="x_plane", align_bytes=64)
+        nc.vector.tensor_copy(x_plane[:], x_byte_table[:].indirect(offs_t[:]))
+        d_picked = keep.tile([P, H], U32, name="d_picked", tag="picked")
+        nc.vector.tensor_copy(d_picked[:], d_word_table[:].indirect(kidx_t[:]))
+        d_codes = keep.tile([P, H], U32, name="d_codes", align_bytes=64)
+        nc.vector.tensor_copy(d_codes[:].rearrange("p (t m) -> p m t", t=PACK), d_picked[:].rearrange("p (m t) -> p m t", t=PACK))
+        x_codes = keep.tile([P, S], U32, name="x_codes", align_bytes=64)
+        halves = [(0, S // 2), (S // 2, S)]
+        for a, b in halves:
+            nc.vector.tensor_copy(x_codes[:, a:b], x_word_table[:].indirect(entries(offs_t, a, b)))
+
+        s_ps = [psum.tile([P, S], F32, name=f"s_ps{t}") for t in range(PACK)]
+        h_ps = [psum.tile([P, S], F32, name=f"h_ps{t}") for t in range(PACK)]
+
+        def scores(t, a, b):
+            cols = slice(t * P, (t + 1) * P)
+            nc.tensor.matmul_mx(out=s_ps[t][:, a:b], lhsT=d_codes[:, cols].bitcast(FP8X4), lhsT_scale=d_plane[:, cols],
+                                rhs=x_codes[:, a:b].bitcast(FP8X4), rhs_scale=x_plane[:, a:b], start=True, stop=True)
+            nc.scalar.activation(s_win[t][:, a:b], s_ps[t][:, a:b], ACT.Copy, scale=-0.0625)
+            nc.scalar.activation(s_own[t][:, a:b], s_ps[t][:, a:b], ACT.Copy, scale=-0.0625)
+
+        for a, b in halves:
+            scores(0, a, b)
+        for t in range(1, PACK):
+            scores(t, 0, S)
+
+        w_raw = keep.tile([P, PACK, N], F32, name="w_raw", tag="big")
+        nc.sync.dma_start(w_raw[:], w1.rearrange("(p j) m -> p j m", j=PACK))
+        w_grouped = keep.tile([P, N * PACK], BF16, name="w_grouped", align_bytes=64)
+        w_codes = keep.tile([P, N], U32, name="w_codes", align_bytes=64)
+        w_plane = keep.tile([P, N], U8, name="w_plane", align_bytes=64)
+
+        def cast_w(part, parts):
+            ms = slice(part * P // parts, (part + 1) * P // parts)
+            nc.scalar.copy(w_grouped[:].rearrange("p (t m j) -> p m t j", t=PACK, j=PACK)[:, ms],
+                           w_raw[:].rearrange("p j (m t) -> p m t j", t=PACK)[:, ms])
+
+        v = [keep.tile([P, S], F32, name=f"v{t}") for t in range(PACK)]
+        low = [keep.tile([P, S], F32, name=f"low{t}") for t in range(PACK)]
+        z_grouped = keep.tile([P, S, PACK], BF16, name="z_grouped", align_bytes=64)
+        z_codes = keep.tile([P, S], U32, name="z_codes", align_bytes=64)
+        z_plane = keep.tile([P, S], U8, name="z_plane", align_bytes=64)
+
+        def step_e(t, a, b):
+            nc.vector.tensor_tensor(e[t][:, a:b], s_win[t][:].indirect(entries(n1_t, a, b)), s_own[t][:, a:b], ALU.add)
+
+        def step_uv(t, a, b):
+            nc.vector.tensor_tensor(u[t][:, a:b], s_win[t][:].indirect(entries(n2_t, a, b)), e[t][:, a:b], ALU.subtract)
+            nc.vector.tensor_tensor(v[t][:, a:b], s_win[t][:].indirect(entries(n3_t, a, b)), e[t][:, a:b], ALU.subtract)
+
+        def step_z(t, a, b):
+            nc.vector.tensor_tensor(low[t][:, a:b], u[t][:, a:b], v[t][:, a:b], ALU.min)
+            nc.scalar.activation(z_grouped[:, a:b, t], low[t][:, a:b], ACT.Copy, scale=gn_t[:, t : t + 1])
+
+        a_own = [keep.tile([P, S], F32, name=f"a_own{t}") for t in range(PACK)]
+
+        def empty_h(t, a, b):
+            nc.scalar.activation(a_win[t][:, a:b], h_ps[t][:, a:b], ACT.Abs)
+            nc.scalar.activation(a_own[t][:, a:b], h_ps[t][:, a:b], ACT.Abs)
+            nc.scalar.copy(h_win[t][:, a:b], h_ps[t][:, a:b])
+
+        def second(a, b):
+            nc.vector.quantize_mx(out=z_codes[:, a:b].bitcast(FP8X4), scales=z_plane[:, a:b],
+                                  in_=z_grouped[:, a:b, :].rearrange("p c t -> p (c t)"))
+            for t in range(PACK):
+                cols = slice(t * P, (t + 1) * P)
+                nc.tensor.matmul_mx(out=h_ps[t][:, a:b], lhsT=w_codes[:, cols].bitcast(FP8X4), lhsT_scale=w_plane[:, cols],
+                                    rhs=z_codes[:, a:b].bitcast(FP8X4), rhs_scale=z_plane[:, a:b], start=True, stop=True)
+            empty_h(0, a, b)
+
+        for a, b in halves:
+            step_e(0, a, b)
+        step_e(1, 0, S)
+        for a, b in halves:
+            step_uv(0, a, b)
+        step_e(2, 0, S)
+        step_z(0, 0, S)
+        for part in range(4):
+            cast_w(part, 4)
+        step_uv(1, 0, S)
+        for a, b in halves:
+            step_e(last, a, b)
+        step_z(1, 0, S)
+        step_uv(2, 0, S)
+        nc.vector.quantize_mx(out=w_codes[:].bitcast(FP8X4), scales=w_plane[:], in_=w_grouped[:])
+        step_z(2, 0, S)
+        pieces = [(0, 256), (256, 384), (384, 512)]
+        step_uv(last, *pieces[0])
+        for i, piece in enumerate(pieces):
+            if i + 1 < len(pieces):
+                step_uv(last, *pieces[i + 1])
+            step_z(last, *piece)
+            if i > 0:
+                second(*pieces[i - 1])
+        second(*pieces[-1])
+
+        den = [keep.tile([P, S], F32, name=f"den{t}") for t in range(PACK)]
+        root = [keep.tile([P, S], F32, name=f"root{t}") for t in range(PACK)]
+        inv = [keep.tile([P, S], F32, name=f"inv{t}") for t in range(PACK)]
+        res = [keep.tile([P, S], F32, name=f"res{t}") for t in range(PACK)]
+        out_rows = out.rearrange("(p t) j -> p t j", t=PACK)
+
+        def step_den(t):
+            nc.vector.tensor_tensor(den[t][:], a_win[t][:].indirect(n5_t[:]), a_own[t][:], ALU.add)
+            nc.scalar.activation(root[t][:], den[t][:], ACT.Abs_reciprocal_sqrt, bias=0.5)
+            nc.scalar.activation(inv[t][:], root[t][:], ACT.Square)
+
+        def step_out(t, a, b):
+            nc.vector.tensor_tensor(res[t][:, a:b], h_win[t][:].indirect(entries(n4_t, a, b)), inv[t][:, a:b], ALU.mult)
+            nc.sync.dma_start(out_rows[:, t, a:b], res[t][:, a:b])
+
+        empty_h(1, 0, S)
+        step_den(0)
+        for t in range(1, PACK):
+            if t + 1 < PACK:
+                empty_h(t + 1, 0, S)
+            step_den(t)
+            step_out(t - 1, 0, S)
+        for a, b in halves:
+            step_out(last, a, b)

@@ -24,6 +24,7 @@ def tile_picked_keytrimnorm2_none_p_kernel(tc, x_words, x_scales, d_words, d_sca
     nc = tc.nc
     with ExitStack() as ctx:
         keep = ctx.enter_context(tc.tile_pool(name="keep", bufs=1))
+        ring = ctx.enter_context(tc.tile_pool(name="ring", bufs=2))
         psum = ctx.enter_context(tc.psum_pool(name="psum", bufs=1))
 
         def load_list(src, name):
@@ -34,143 +35,159 @@ def tile_picked_keytrimnorm2_none_p_kernel(tc, x_words, x_scales, d_words, d_sca
         def entries(lst, a, b):
             return lst[:, a // STRIPE : b // STRIPE]
 
+        last = PACK - 1
+        HALF = S // 2
+        halves = [(0, HALF), (HALF, S)]
+
         d_byte_table = keep.tile([P, G], U8, name="d_byte_table")
         x_byte_table = keep.tile([P, T], U8, name="x_byte_table")
-        d_plane = keep.tile([P, H], U8, name="d_plane", align_bytes=64)
-        nc.gpsimd.memset(d_byte_table[:].bitcast(I32), 0)
-        nc.vector.memset(x_byte_table[:].bitcast(I32), 0)
-        nc.gpsimd.memset(d_plane[:].bitcast(I32), 0)
+        nc.vector.memset(d_byte_table[:].bitcast(I32), 0)
+        nc.gpsimd.memset(x_byte_table[:].bitcast(I32), 0)
+        nc.scalar.dma_start(d_byte_table[0:P:8, :].bitcast(I32), d_scales[0].bitcast(I32))
+        nc.gpsimd.dma_start(x_byte_table[0:P:8, :].bitcast(I32), x_scales[0].bitcast(I32))
+        gn_t = keep.tile([P, PACK], F32, name="gn_t")
+        nc.gpsimd.dma_start(gn_t[:], gn.rearrange("(p t) o -> p (t o)", t=PACK))
 
         kidx_t = load_list(kidx, "kidx_t")
-        nc.scalar.dma_start(d_byte_table[0:P:8, :].bitcast(I32), d_scales[0].bitcast(I32))
-        d_word_table = keep.tile([P, G], U32, name="d_word_table")
+        d_word_table = keep.tile([P, G], U32, name="d_word_table", tag="table")
         nc.sync.dma_start(d_word_table[:].bitcast(I32), d_words[0].rearrange("p c r -> p (c r)").bitcast(I32))
         offs_t = load_list(offs, "offs_t")
-        x_word_table = keep.tile([P, T], U32, name="x_word_table", tag="big")
-        nc.sync.dma_start(x_word_table[:].bitcast(I32), x_words[0].rearrange("p c r -> p (c r)").bitcast(I32))
-        for q in range(4):
-            nc.scalar.dma_start(x_byte_table[32 * q : 32 * q + 4, :].bitcast(I32), x_scales[0, 4 * q : 4 * q + 4, :].bitcast(I32))
         n1_t = load_list(n1, "n1_t")
         n2_t = load_list(n2, "n2_t")
         n3_t = load_list(n3, "n3_t")
-        gn_t = keep.tile([P, PACK], F32, name="gn_t")
-        nc.sync.dma_start(gn_t[:], gn.rearrange("(p t) o -> p (t o)", t=PACK))
         n5_t = load_list(n5, "n5_t")
+        x_word_table = keep.tile([P, T], U32, name="x_word_table")
+        nc.sync.dma_start(x_word_table[:].bitcast(I32), x_words[0].rearrange("p c r -> p (c r)").bitcast(I32))
         n4_t = load_list(n4, "n4_t")
 
-        warm = keep.tile([P, 1], F32, name="warm")
-        nc.scalar.activation(warm[:], gn_t[:, 0:1], ACT.Abs_reciprocal_sqrt, scale=0.0, bias=1.0)
+        warm = keep.tile([P, 2], F32, name="warm")
+        nc.vector.memset(warm[:, 0:1], 1.0)
+        nc.scalar.activation(warm[:, 1:2], warm[:, 0:1], ACT.Abs_reciprocal_sqrt)
 
-        last = PACK - 1
-        s_win = [keep.tile([P, S if t in (0, last) else 2 * S], F32, name=f"s_win{t}") for t in range(PACK)]
-        h_win = [keep.tile([P, 2 * S], F32, name=f"h_win{t}") for t in range(PACK)]
-        a_win = [keep.tile([P, 2 * S], F32, name=f"a_win{t}") for t in range(PACK)]
-        s_own = [s_win[t + 1][:, S:] for t in range(last - 1)]
-        s_own.extend(keep.tile([P, S], F32, name=f"s_own{t}")[:] for t in (last - 1, last))
-        e = [a_win[t][:, S:] for t in range(PACK)]
-        u = [h_win[t][:, S:] for t in range(PACK)]
+        def rows_to_plane(queue, plane):
+            for r in range(1, 4):
+                queue.dma_start(plane[r:P:32, :].bitcast(I32), plane[8 * r : P : 32, :].bitcast(I32))
 
         d_bytes = keep.tile([P, H], U8, name="d_bytes", tag="picked")
         nc.vector.tensor_copy(d_bytes[:], d_byte_table[:].indirect(kidx_t[:]))
-        d_bytes_dealt = keep.tile([P, H], U8, name="d_bytes_dealt")
-        nc.vector.tensor_copy(d_bytes_dealt[:].rearrange("p (t m) -> p t m", t=PACK), d_bytes[:].rearrange("p (m t) -> p t m", t=PACK))
-        for r in range(4):
-            nc.sync.dma_start(d_plane[r:P:32, :].bitcast(I32), d_bytes_dealt[8 * r : P : 32, :].bitcast(I32))
+        x_bytes = keep.tile([P, S], U8, name="x_bytes")
+        nc.vector.tensor_copy(x_bytes[:], x_byte_table[:].indirect(offs_t[:]))
+        d_plane = keep.tile([P, H], U8, name="d_plane", align_bytes=64)
+        nc.vector.tensor_copy(d_plane[:].rearrange("p (t m) -> p t m", t=PACK), d_bytes[:].rearrange("p (m t) -> p t m", t=PACK))
+        rows_to_plane(nc.scalar, d_plane)
         x_plane = keep.tile([P, S], U8, name="x_plane", align_bytes=64)
-        nc.vector.tensor_copy(x_plane[:], x_byte_table[:].indirect(offs_t[:]))
+        nc.vector.tensor_copy(x_plane[:].bitcast(I32), x_bytes[:].bitcast(I32))
+        rows_to_plane(nc.sync, x_plane)
         d_picked = keep.tile([P, H], U32, name="d_picked", tag="picked")
         nc.vector.tensor_copy(d_picked[:], d_word_table[:].indirect(kidx_t[:]))
-        d_codes = keep.tile([P, H], U32, name="d_codes", align_bytes=64)
-        nc.vector.tensor_copy(d_codes[:].rearrange("p (t m) -> p m t", t=PACK), d_picked[:].rearrange("p (m t) -> p m t", t=PACK))
         x_codes = keep.tile([P, S], U32, name="x_codes", align_bytes=64)
-        halves = [(0, S // 2), (S // 2, S)]
-        for a, b in halves:
-            nc.vector.tensor_copy(x_codes[:, a:b], x_word_table[:].indirect(entries(offs_t, a, b)))
+        nc.vector.tensor_copy(x_codes[:, :HALF], x_word_table[:].indirect(entries(offs_t, 0, HALF)))
+        d_codes = keep.tile([P, H], U32, name="d_codes", align_bytes=64)
+        dealt = d_codes[:].rearrange("p (t m) -> p m t", t=PACK)
+        picked = d_picked[:].rearrange("p (m t) -> p m t", t=PACK)
+        nc.vector.tensor_copy(dealt[:, :, 0], picked[:, :, 0])
+        nc.vector.tensor_copy(x_codes[:, HALF:], x_word_table[:].indirect(entries(offs_t, HALF, S)))
+        nc.vector.tensor_copy(dealt[:, :, 1:], picked[:, :, 1:])
+
+        w_raw = keep.tile([P, PACK, N], F32, name="w_raw", tag="table")
+        nc.sync.dma_start(w_raw[:], w1.rearrange("(p j) m -> p j m", j=PACK))
 
         s_ps = [psum.tile([P, S], F32, name=f"s_ps{t}") for t in range(PACK)]
         h_ps = [psum.tile([P, S], F32, name=f"h_ps{t}") for t in range(PACK)]
+        s_win = [keep.tile([P, S], F32, name=f"s_win{t}") for t in range(PACK)]
+        h_win = [keep.tile([P, 2 * S], F32, name=f"h_win{t}") for t in range(PACK)]
+        a_win = [keep.tile([P, 2 * S], F32, name=f"a_win{t}") for t in range(PACK)]
+        s_own = [h_win[t][:, S:] for t in range(PACK)]
+        low = [a_win[t][:, S:] for t in range(PACK)]
+        a_own = [keep.tile([P, S], F32, name=f"a_own{t}") for t in range(PACK)]
 
-        def scores(t, a, b):
+        def product(bank, t, lhs, lhs_plane, rhs, rhs_plane, a, b):
             cols = slice(t * P, (t + 1) * P)
-            nc.tensor.matmul_mx(out=s_ps[t][:, a:b], lhsT=d_codes[:, cols].bitcast(FP8X4), lhsT_scale=d_plane[:, cols],
-                                rhs=x_codes[:, a:b].bitcast(FP8X4), rhs_scale=x_plane[:, a:b], start=True, stop=True)
-            nc.scalar.activation(s_win[t][:, a:b], s_ps[t][:, a:b], ACT.Copy, scale=-0.0625)
-            nc.scalar.activation(s_own[t][:, a:b], s_ps[t][:, a:b], ACT.Copy, scale=-0.0625)
+            nc.tensor.matmul_mx(out=bank[:, a:b], lhsT=lhs[:, cols].bitcast(FP8X4), lhsT_scale=lhs_plane[:, cols],
+                                rhs=rhs[:, a:b].bitcast(FP8X4), rhs_scale=rhs_plane[:, a:b], start=True, stop=True)
+
+        def empty_s(dst, t, a, b):
+            nc.scalar.activation(dst[t][:, a:b], s_ps[t][:, a:b], ACT.Copy, scale=-0.0625)
 
         for a, b in halves:
-            scores(0, a, b)
+            product(s_ps[0], 0, d_codes, d_plane, x_codes, x_plane, a, b)
+            empty_s(s_win, 0, a, b)
+            if a == 0:
+                empty_s(s_own, 0, 0, HALF)
         for t in range(1, PACK):
-            scores(t, 0, S)
+            product(s_ps[t], t, d_codes, d_plane, x_codes, x_plane, 0, S)
+            empty_s(s_win, t, 0, S)
+            empty_s(s_own, t, 0, HALF)
+        for t in range(PACK):
+            nc.sync.dma_start(s_own[t][:, HALF:], s_win[t][:, HALF:])
 
-        w_raw = keep.tile([P, PACK, N], F32, name="w_raw", tag="big")
-        nc.sync.dma_start(w_raw[:], w1.rearrange("(p j) m -> p j m", j=PACK))
         w_grouped = keep.tile([P, N * PACK], BF16, name="w_grouped", align_bytes=64)
         w_codes = keep.tile([P, N], U32, name="w_codes", align_bytes=64)
         w_plane = keep.tile([P, N], U8, name="w_plane", align_bytes=64)
 
-        def cast_w(part, parts):
-            ms = slice(part * P // parts, (part + 1) * P // parts)
+        def cast_w(part):
+            ms = slice(part * P // PACK, (part + 1) * P // PACK)
             nc.scalar.copy(w_grouped[:].rearrange("p (t m j) -> p m t j", t=PACK, j=PACK)[:, ms],
                            w_raw[:].rearrange("p j (m t) -> p m t j", t=PACK)[:, ms])
 
-        v = [keep.tile([P, S], F32, name=f"v{t}") for t in range(PACK)]
-        low = [keep.tile([P, S], F32, name=f"low{t}") for t in range(PACK)]
         z_grouped = keep.tile([P, S, PACK], BF16, name="z_grouped", align_bytes=64)
         z_codes = keep.tile([P, S], U32, name="z_codes", align_bytes=64)
         z_plane = keep.tile([P, S], U8, name="z_plane", align_bytes=64)
 
-        def step_e(t, a, b):
-            nc.vector.tensor_tensor(e[t][:, a:b], s_win[t][:].indirect(entries(n1_t, a, b)), s_own[t][:, a:b], ALU.add)
+        steps = [(t, a, b) for a, b in halves for t in range(PACK)]
+        steps[-1:] = [(last, HALF, HALF + P), (last, HALF + P, S)]
+        e, u, v = {}, {}, {}
 
-        def step_uv(t, a, b):
-            nc.vector.tensor_tensor(u[t][:, a:b], s_win[t][:].indirect(entries(n2_t, a, b)), e[t][:, a:b], ALU.subtract)
-            nc.vector.tensor_tensor(v[t][:, a:b], s_win[t][:].indirect(entries(n3_t, a, b)), e[t][:, a:b], ALU.subtract)
+        def step_e(k):
+            t, a, b = steps[k]
+            e[k] = ring.tile([P, b - a], F32, name="e", bufs=3)
+            nc.vector.tensor_tensor(e[k][:], s_win[t][:].indirect(entries(n1_t, a, b)), s_own[t][:, a:b], ALU.add)
 
-        def step_z(t, a, b):
-            nc.vector.tensor_tensor(low[t][:, a:b], u[t][:, a:b], v[t][:, a:b], ALU.min)
+        def step_uv(k):
+            t, a, b = steps[k]
+            u[k] = ring.tile([P, b - a], F32, name="u")
+            v[k] = ring.tile([P, b - a], F32, name="v")
+            nc.vector.tensor_tensor(u[k][:], s_win[t][:].indirect(entries(n2_t, a, b)), e[k][:], ALU.subtract)
+            nc.vector.tensor_tensor(v[k][:], s_win[t][:].indirect(entries(n3_t, a, b)), e[k][:], ALU.subtract)
+
+        def step_z(k):
+            t, a, b = steps[k]
+            nc.vector.tensor_tensor(low[t][:, a:b], u[k][:], v[k][:], ALU.min)
             nc.scalar.activation(z_grouped[:, a:b, t], low[t][:, a:b], ACT.Copy, scale=gn_t[:, t : t + 1])
-
-        a_own = [keep.tile([P, S], F32, name=f"a_own{t}") for t in range(PACK)]
-
-        def empty_h(t, a, b):
-            nc.scalar.activation(a_win[t][:, a:b], h_ps[t][:, a:b], ACT.Abs)
-            nc.scalar.activation(a_own[t][:, a:b], h_ps[t][:, a:b], ACT.Abs)
-            nc.scalar.copy(h_win[t][:, a:b], h_ps[t][:, a:b])
 
         def second(a, b):
             nc.vector.quantize_mx(out=z_codes[:, a:b].bitcast(FP8X4), scales=z_plane[:, a:b],
                                   in_=z_grouped[:, a:b, :].rearrange("p c t -> p (c t)"))
             for t in range(PACK):
-                cols = slice(t * P, (t + 1) * P)
-                nc.tensor.matmul_mx(out=h_ps[t][:, a:b], lhsT=w_codes[:, cols].bitcast(FP8X4), lhsT_scale=w_plane[:, cols],
-                                    rhs=z_codes[:, a:b].bitcast(FP8X4), rhs_scale=z_plane[:, a:b], start=True, stop=True)
-            empty_h(0, a, b)
+                product(h_ps[t], t, w_codes, w_plane, z_codes, z_plane, a, b)
 
-        for a, b in halves:
-            step_e(0, a, b)
-        step_e(1, 0, S)
-        for a, b in halves:
-            step_uv(0, a, b)
-        step_e(2, 0, S)
-        step_z(0, 0, S)
-        for part in range(4):
-            cast_w(part, 4)
-        step_uv(1, 0, S)
-        for a, b in halves:
-            step_e(last, a, b)
-        step_z(1, 0, S)
-        step_uv(2, 0, S)
-        nc.vector.quantize_mx(out=w_codes[:].bitcast(FP8X4), scales=w_plane[:], in_=w_grouped[:])
-        step_z(2, 0, S)
-        pieces = [(0, 256), (256, 384), (384, 512)]
-        step_uv(last, *pieces[0])
-        for i, piece in enumerate(pieces):
-            if i + 1 < len(pieces):
-                step_uv(last, *pieces[i + 1])
-            step_z(last, *piece)
-            if i > 0:
-                second(*pieces[i - 1])
-        second(*pieces[-1])
+        def empty_abs(dst, t, a, b):
+            nc.scalar.activation(dst[t][:, a:b], h_ps[t][:, a:b], ACT.Abs)
+
+        def empty_h(t, a, b):
+            nc.scalar.copy(h_win[t][:, a:b], h_ps[t][:, a:b])
+
+        def first_half_out(t):
+            empty_abs(a_win, t, 0, HALF)
+            nc.sync.dma_start(a_own[t][:, :HALF], a_win[t][:, :HALF])
+            empty_h(t, 0, HALF)
+
+        step_e(0)
+        step_e(1)
+        for k in range(len(steps)):
+            step_uv(k)
+            if k + 2 < len(steps):
+                step_e(k + 2)
+            if k < PACK:
+                cast_w(k)
+            if k == PACK:
+                nc.vector.quantize_mx(out=w_codes[:].bitcast(FP8X4), scales=w_plane[:], in_=w_grouped[:])
+                second(0, HALF)
+            step_z(k)
+            if PACK <= k < 2 * PACK:
+                first_half_out(k - PACK)
+        second(HALF, HALF + P)
+        second(HALF + P, S)
 
         den = [keep.tile([P, S], F32, name=f"den{t}") for t in range(PACK)]
         root = [keep.tile([P, S], F32, name=f"root{t}") for t in range(PACK)]
@@ -178,21 +195,25 @@ def tile_picked_keytrimnorm2_none_p_kernel(tc, x_words, x_scales, d_words, d_sca
         res = [keep.tile([P, S], F32, name=f"res{t}") for t in range(PACK)]
         out_rows = out.rearrange("(p t) j -> p t j", t=PACK)
 
-        def step_den(t):
+        def step_den(t, pieces):
+            for a, b in pieces:
+                empty_abs(a_win, t, a, b)
+                empty_abs(a_own, t, a, b)
             nc.vector.tensor_tensor(den[t][:], a_win[t][:].indirect(n5_t[:]), a_own[t][:], ALU.add)
+
+        def step_out(t, pieces):
             nc.scalar.activation(root[t][:], den[t][:], ACT.Abs_reciprocal_sqrt, bias=0.5)
             nc.scalar.activation(inv[t][:], root[t][:], ACT.Square)
+            empty_h(t, HALF, S)
+            for a, b in pieces:
+                nc.vector.tensor_tensor(res[t][:, a:b], h_win[t][:].indirect(entries(n4_t, a, b)), inv[t][:, a:b], ALU.mult)
+                nc.sync.dma_start(out_rows[:, t, a:b], res[t][:, a:b])
 
-        def step_out(t, a, b):
-            nc.vector.tensor_tensor(res[t][:, a:b], h_win[t][:].indirect(entries(n4_t, a, b)), inv[t][:, a:b], ALU.mult)
-            nc.sync.dma_start(out_rows[:, t, a:b], res[t][:, a:b])
-
-        empty_h(1, 0, S)
-        step_den(0)
-        for t in range(1, PACK):
-            if t + 1 < PACK:
-                empty_h(t + 1, 0, S)
-            step_den(t)
-            step_out(t - 1, 0, S)
-        for a, b in halves:
-            step_out(last, a, b)
+        step_den(0, [(HALF, HALF + P), (HALF + P, S)])
+        step_den(1, halves[1:])
+        step_den(2, halves[1:])
+        step_out(0, [(0, S)])
+        step_den(3, halves[1:])
+        step_out(1, [(0, S)])
+        step_out(2, [(0, S)])
+        step_out(3, halves)

@@ -18,6 +18,7 @@ ACT = mybir.ActivationFunctionType
 P = 128
 PACK = 4
 STRIPE = 16
+X_ZERO_SPLIT = 768
 
 
 def tile_picked_keytrimnorm2_none_p_kernel(tc, x_words, x_scales, d_words, d_scales, gn, w1, offs, kidx, n1, n2, n3, n4, n5, out):
@@ -40,57 +41,59 @@ def tile_picked_keytrimnorm2_none_p_kernel(tc, x_words, x_scales, d_words, d_sca
         halves = [(0, HALF), (HALF, S)]
 
         d_byte_table = keep.tile([P, G], U8, name="d_byte_table")
-        x_byte_table = keep.tile([P, T], U8, name="x_byte_table")
+        x_byte_table = keep.tile([P, T], U8, name="x_byte_table", tag="picked")
         nc.vector.memset(d_byte_table[:].bitcast(I32), 0)
-        nc.gpsimd.memset(x_byte_table[:].bitcast(I32), 0)
-        nc.scalar.dma_start(d_byte_table[0:P:8, :].bitcast(I32), d_scales[0].bitcast(I32))
-        nc.gpsimd.dma_start(x_byte_table[0:P:8, :].bitcast(I32), x_scales[0].bitcast(I32))
-        gn_t = keep.tile([P, PACK], F32, name="gn_t")
-        nc.gpsimd.dma_start(gn_t[:], gn.rearrange("(p t) o -> p (t o)", t=PACK))
+        nc.vector.memset(x_byte_table[:, :X_ZERO_SPLIT].bitcast(I32), 0)
+        nc.gpsimd.memset(x_byte_table[:, X_ZERO_SPLIT:].bitcast(I32), 0)
+        planes = keep.tile([P, H + S], U8, name="planes", align_bytes=64)
+        nc.gpsimd.memset(planes[:].bitcast(I32), 0)
 
         kidx_t = load_list(kidx, "kidx_t")
-        d_word_table = keep.tile([P, G], U32, name="d_word_table", tag="table")
-        nc.sync.dma_start(d_word_table[:].bitcast(I32), d_words[0].rearrange("p c r -> p (c r)").bitcast(I32))
         offs_t = load_list(offs, "offs_t")
+        nc.sync.dma_start(d_byte_table[0:P:8, :].bitcast(I32), d_scales[0].bitcast(I32))
         n1_t = load_list(n1, "n1_t")
         n2_t = load_list(n2, "n2_t")
         n3_t = load_list(n3, "n3_t")
+        nc.sync.dma_start(x_byte_table[0:P:8, :].bitcast(I32), x_scales[0].bitcast(I32))
+        d_word_table = keep.tile([P, G], U32, name="d_word_table")
+        nc.sync.dma_start(d_word_table[:].bitcast(I32), d_words[0].rearrange("p c r -> p (c r)").bitcast(I32))
         n5_t = load_list(n5, "n5_t")
-        x_word_table = keep.tile([P, T], U32, name="x_word_table")
-        nc.sync.dma_start(x_word_table[:].bitcast(I32), x_words[0].rearrange("p c r -> p (c r)").bitcast(I32))
         n4_t = load_list(n4, "n4_t")
+        x_word_table = keep.tile([P, T], U32, name="x_word_table", tag="table")
+        nc.sync.dma_start(x_word_table[:].bitcast(I32), x_words[0].rearrange("p c r -> p (c r)").bitcast(I32))
 
         warm = keep.tile([P, 2], F32, name="warm")
         nc.vector.memset(warm[:, 0:1], 1.0)
         nc.scalar.activation(warm[:, 1:2], warm[:, 0:1], ACT.Abs_reciprocal_sqrt)
 
-        def rows_to_plane(queue, plane):
-            for r in range(1, 4):
-                queue.dma_start(plane[r:P:32, :].bitcast(I32), plane[8 * r : P : 32, :].bitcast(I32))
-
-        d_bytes = keep.tile([P, H], U8, name="d_bytes", tag="picked")
+        d_bytes = keep.tile([P, H], U8, name="d_bytes")
         nc.vector.tensor_copy(d_bytes[:], d_byte_table[:].indirect(kidx_t[:]))
         x_bytes = keep.tile([P, S], U8, name="x_bytes")
         nc.vector.tensor_copy(x_bytes[:], x_byte_table[:].indirect(offs_t[:]))
-        d_plane = keep.tile([P, H], U8, name="d_plane", align_bytes=64)
-        nc.vector.tensor_copy(d_plane[:].rearrange("p (t m) -> p t m", t=PACK), d_bytes[:].rearrange("p (m t) -> p t m", t=PACK))
-        rows_to_plane(nc.scalar, d_plane)
-        x_plane = keep.tile([P, S], U8, name="x_plane", align_bytes=64)
-        nc.vector.tensor_copy(x_plane[:].bitcast(I32), x_bytes[:].bitcast(I32))
-        rows_to_plane(nc.sync, x_plane)
+        spread = keep.tile([P, H + S], U8, name="spread")
+        nc.vector.tensor_copy(spread[:, :H].rearrange("p (t m) -> p t m", t=PACK), d_bytes[:].rearrange("p (m t) -> p t m", t=PACK))
+        nc.vector.tensor_copy(spread[:, H:].bitcast(I32), x_bytes[:].bitcast(I32))
+        for q in range(4):
+            nc.scalar.dma_start(planes[32 * q : 32 * q + 4, :].bitcast(I32), spread[32 * q : 32 * q + 32 : 8, :].bitcast(I32))
+        d_plane = planes[:, :H]
+        x_plane = planes[:, H:]
         d_picked = keep.tile([P, H], U32, name="d_picked", tag="picked")
         nc.vector.tensor_copy(d_picked[:], d_word_table[:].indirect(kidx_t[:]))
         x_codes = keep.tile([P, S], U32, name="x_codes", align_bytes=64)
         nc.vector.tensor_copy(x_codes[:, :HALF], x_word_table[:].indirect(entries(offs_t, 0, HALF)))
-        d_codes = keep.tile([P, H], U32, name="d_codes", align_bytes=64)
-        dealt = d_codes[:].rearrange("p (t m) -> p m t", t=PACK)
+        d_first = keep.tile([P, P], U32, name="d_first", align_bytes=64)
+        d_rest = keep.tile([P, PACK - 1, P], U32, name="d_rest", align_bytes=64)
+        d_codes = [d_first[:]] + [d_rest[:, t, :] for t in range(PACK - 1)]
         picked = d_picked[:].rearrange("p (m t) -> p m t", t=PACK)
-        nc.vector.tensor_copy(dealt[:, :, 0], picked[:, :, 0])
+        nc.vector.tensor_copy(d_first[:], picked[:, :, 0])
         nc.vector.tensor_copy(x_codes[:, HALF:], x_word_table[:].indirect(entries(offs_t, HALF, S)))
-        nc.vector.tensor_copy(dealt[:, :, 1:], picked[:, :, 1:])
+        nc.vector.tensor_copy(d_rest[:].rearrange("p t m -> p m t"), picked[:, :, 1:])
 
         w_raw = keep.tile([P, PACK, N], F32, name="w_raw", tag="table")
         nc.sync.dma_start(w_raw[:], w1.rearrange("(p j) m -> p j m", j=PACK))
+
+        gn_t = keep.tile([P, PACK], F32, name="gn_t", tag="picked")
+        nc.sync.dma_start(gn_t[:], gn.rearrange("(p t) o -> p (t o)", t=PACK))
 
         s_ps = [psum.tile([P, S], F32, name=f"s_ps{t}") for t in range(PACK)]
         h_ps = [psum.tile([P, S], F32, name=f"h_ps{t}") for t in range(PACK)]
@@ -103,19 +106,22 @@ def tile_picked_keytrimnorm2_none_p_kernel(tc, x_words, x_scales, d_words, d_sca
 
         def product(bank, t, lhs, lhs_plane, rhs, rhs_plane, a, b):
             cols = slice(t * P, (t + 1) * P)
-            nc.tensor.matmul_mx(out=bank[:, a:b], lhsT=lhs[:, cols].bitcast(FP8X4), lhsT_scale=lhs_plane[:, cols],
+            nc.tensor.matmul_mx(out=bank[:, a:b], lhsT=lhs.bitcast(FP8X4), lhsT_scale=lhs_plane[:, cols],
                                 rhs=rhs[:, a:b].bitcast(FP8X4), rhs_scale=rhs_plane[:, a:b], start=True, stop=True)
 
         def empty_s(dst, t, a, b):
-            nc.scalar.activation(dst[t][:, a:b], s_ps[t][:, a:b], ACT.Copy, scale=-0.0625)
+            bank = h_ps[0] if (t, b) == (0, HALF) else s_ps[t]
+            nc.scalar.activation(dst[t][:, a:b], bank[:, a:b], ACT.Copy, scale=-0.0625)
 
-        for a, b in halves:
-            product(s_ps[0], 0, d_codes, d_plane, x_codes, x_plane, a, b)
-            empty_s(s_win, 0, a, b)
+        for bank, (a, b) in zip((h_ps[0], s_ps[0]), halves):
+            product(bank, 0, d_codes[0], d_plane, x_codes, x_plane, a, b)
             if a == 0:
-                empty_s(s_own, 0, 0, HALF)
+                empty_s(s_win, 0, a, b)
+                empty_s(s_own, 0, a, b)
+            else:
+                nc.vector.tensor_scalar(s_win[0][:, a:b], bank[:, a:b], -0.0625, None, ALU.mult)
         for t in range(1, PACK):
-            product(s_ps[t], t, d_codes, d_plane, x_codes, x_plane, 0, S)
+            product(s_ps[t], t, d_codes[t], d_plane, x_codes, x_plane, 0, S)
             empty_s(s_win, t, 0, S)
             empty_s(s_own, t, 0, HALF)
         for t in range(PACK):
@@ -155,17 +161,21 @@ def tile_picked_keytrimnorm2_none_p_kernel(tc, x_words, x_scales, d_words, d_sca
             nc.vector.tensor_tensor(low[t][:, a:b], u[k][:], v[k][:], ALU.min)
             nc.scalar.activation(z_grouped[:, a:b, t], low[t][:, a:b], ACT.Copy, scale=gn_t[:, t : t + 1])
 
+        def h_bank(t, a, b):
+            early = b <= HALF or (t, b) == (0, HALF + P)
+            return (h_ps if early else s_ps)[t]
+
         def second(a, b):
             nc.vector.quantize_mx(out=z_codes[:, a:b].bitcast(FP8X4), scales=z_plane[:, a:b],
                                   in_=z_grouped[:, a:b, :].rearrange("p c t -> p (c t)"))
             for t in range(PACK):
-                product(h_ps[t], t, w_codes, w_plane, z_codes, z_plane, a, b)
+                product(h_bank(t, a, b), t, w_codes[:, t * P : (t + 1) * P], w_plane, z_codes, z_plane, a, b)
 
         def empty_abs(dst, t, a, b):
-            nc.scalar.activation(dst[t][:, a:b], h_ps[t][:, a:b], ACT.Abs)
+            nc.scalar.activation(dst[t][:, a:b], h_bank(t, a, b)[:, a:b], ACT.Abs)
 
         def empty_h(t, a, b):
-            nc.scalar.copy(h_win[t][:, a:b], h_ps[t][:, a:b])
+            nc.scalar.copy(h_win[t][:, a:b], h_bank(t, a, b)[:, a:b])
 
         def first_half_out(t):
             empty_abs(a_win, t, 0, HALF)
@@ -204,16 +214,18 @@ def tile_picked_keytrimnorm2_none_p_kernel(tc, x_words, x_scales, d_words, d_sca
         def step_out(t, pieces):
             nc.scalar.activation(root[t][:], den[t][:], ACT.Abs_reciprocal_sqrt, bias=0.5)
             nc.scalar.activation(inv[t][:], root[t][:], ACT.Square)
-            empty_h(t, HALF, S)
+            for a, b in steps_b if t == 0 else halves[1:]:
+                empty_h(t, a, b)
             for a, b in pieces:
                 nc.vector.tensor_tensor(res[t][:, a:b], h_win[t][:].indirect(entries(n4_t, a, b)), inv[t][:, a:b], ALU.mult)
                 nc.sync.dma_start(out_rows[:, t, a:b], res[t][:, a:b])
 
-        step_den(0, [(HALF, HALF + P), (HALF + P, S)])
+        steps_b = [(HALF, HALF + P), (HALF + P, S)]
+        step_den(0, steps_b)
         step_den(1, halves[1:])
         step_den(2, halves[1:])
         step_out(0, [(0, S)])
         step_den(3, halves[1:])
         step_out(1, [(0, S)])
         step_out(2, [(0, S)])
-        step_out(3, halves)
+        step_out(3, [(0, S - P), (S - P, S)])

@@ -19,6 +19,7 @@ P = 128
 PACK = 4
 STRIPE = 16
 X_ZERO_SPLIT = 768
+D_EARLY = 512
 
 
 def tile_picked_keytrimnorm2_none_p_kernel(tc, x_words, x_scales, d_words, d_scales, gn, w1, offs, kidx, n1, n2, n3, n4, n5, out):
@@ -48,19 +49,21 @@ def tile_picked_keytrimnorm2_none_p_kernel(tc, x_words, x_scales, d_words, d_sca
         planes = keep.tile([P, H + S], U8, name="planes", align_bytes=64)
         nc.gpsimd.memset(planes[:].bitcast(I32), 0)
 
+        d_word_table = keep.tile([P, G], U32, name="d_word_table")
+        d_word_rows = d_words[0].rearrange("p c r -> p (c r)").bitcast(I32)
+        x_word_table = keep.tile([P, T], U32, name="x_word_table", tag="table")
         kidx_t = load_list(kidx, "kidx_t")
+        nc.sync.dma_start(d_word_table[:, :D_EARLY].bitcast(I32), d_word_rows[:, :D_EARLY])
         offs_t = load_list(offs, "offs_t")
         nc.sync.dma_start(d_byte_table[0:P:8, :].bitcast(I32), d_scales[0].bitcast(I32))
         n1_t = load_list(n1, "n1_t")
         n2_t = load_list(n2, "n2_t")
-        n3_t = load_list(n3, "n3_t")
         nc.sync.dma_start(x_byte_table[0:P:8, :].bitcast(I32), x_scales[0].bitcast(I32))
-        d_word_table = keep.tile([P, G], U32, name="d_word_table")
-        nc.sync.dma_start(d_word_table[:].bitcast(I32), d_words[0].rearrange("p c r -> p (c r)").bitcast(I32))
+        nc.sync.dma_start(d_word_table[:, D_EARLY:].bitcast(I32), d_word_rows[:, D_EARLY:])
+        nc.sync.dma_start(x_word_table[:].bitcast(I32), x_words[0].rearrange("p c r -> p (c r)").bitcast(I32))
+        n3_t = load_list(n3, "n3_t")
         n5_t = load_list(n5, "n5_t")
         n4_t = load_list(n4, "n4_t")
-        x_word_table = keep.tile([P, T], U32, name="x_word_table", tag="table")
-        nc.sync.dma_start(x_word_table[:].bitcast(I32), x_words[0].rearrange("p c r -> p (c r)").bitcast(I32))
 
         warm = keep.tile([P, 2], F32, name="warm")
         nc.vector.memset(warm[:, 0:1], 1.0)
@@ -74,19 +77,19 @@ def tile_picked_keytrimnorm2_none_p_kernel(tc, x_words, x_scales, d_words, d_sca
         nc.vector.tensor_copy(spread[:, :H].rearrange("p (t m) -> p t m", t=PACK), d_bytes[:].rearrange("p (m t) -> p t m", t=PACK))
         nc.vector.tensor_copy(spread[:, H:].bitcast(I32), x_bytes[:].bitcast(I32))
         for q in range(4):
-            nc.scalar.dma_start(planes[32 * q : 32 * q + 4, :].bitcast(I32), spread[32 * q : 32 * q + 32 : 8, :].bitcast(I32))
+            (nc.scalar, nc.sync)[q % 2].dma_start(planes[32 * q : 32 * q + 4, :].bitcast(I32), spread[32 * q : 32 * q + 32 : 8, :].bitcast(I32))
         d_plane = planes[:, :H]
         x_plane = planes[:, H:]
         d_picked = keep.tile([P, H], U32, name="d_picked", tag="picked")
         nc.vector.tensor_copy(d_picked[:], d_word_table[:].indirect(kidx_t[:]))
-        x_codes = keep.tile([P, S], U32, name="x_codes", align_bytes=64)
-        nc.vector.tensor_copy(x_codes[:, :HALF], x_word_table[:].indirect(entries(offs_t, 0, HALF)))
+        x_codes = [keep.tile([P, HALF], U32, name=f"x_codes{i}", align_bytes=64) for i in range(2)]
+        nc.vector.tensor_copy(x_codes[0][:], x_word_table[:].indirect(entries(offs_t, 0, HALF)))
         d_first = keep.tile([P, P], U32, name="d_first", align_bytes=64)
         d_rest = keep.tile([P, PACK - 1, P], U32, name="d_rest", align_bytes=64)
         d_codes = [d_first[:]] + [d_rest[:, t, :] for t in range(PACK - 1)]
         picked = d_picked[:].rearrange("p (m t) -> p m t", t=PACK)
         nc.vector.tensor_copy(d_first[:], picked[:, :, 0])
-        nc.vector.tensor_copy(x_codes[:, HALF:], x_word_table[:].indirect(entries(offs_t, HALF, S)))
+        nc.vector.tensor_copy(x_codes[1][:], x_word_table[:].indirect(entries(offs_t, HALF, S)))
         nc.vector.tensor_copy(d_rest[:].rearrange("p t m -> p m t"), picked[:, :, 1:])
 
         w_raw = keep.tile([P, PACK, N], F32, name="w_raw", tag="table")
@@ -107,21 +110,22 @@ def tile_picked_keytrimnorm2_none_p_kernel(tc, x_words, x_scales, d_words, d_sca
         def product(bank, t, lhs, lhs_plane, rhs, rhs_plane, a, b):
             cols = slice(t * P, (t + 1) * P)
             nc.tensor.matmul_mx(out=bank[:, a:b], lhsT=lhs.bitcast(FP8X4), lhsT_scale=lhs_plane[:, cols],
-                                rhs=rhs[:, a:b].bitcast(FP8X4), rhs_scale=rhs_plane[:, a:b], start=True, stop=True)
+                                rhs=rhs.bitcast(FP8X4), rhs_scale=rhs_plane[:, a:b], start=True, stop=True)
 
         def empty_s(dst, t, a, b):
             bank = h_ps[0] if (t, b) == (0, HALF) else s_ps[t]
             nc.scalar.activation(dst[t][:, a:b], bank[:, a:b], ACT.Copy, scale=-0.0625)
 
         for bank, (a, b) in zip((h_ps[0], s_ps[0]), halves):
-            product(bank, 0, d_codes[0], d_plane, x_codes, x_plane, a, b)
+            product(bank, 0, d_codes[0], d_plane, x_codes[a // HALF][:], x_plane, a, b)
             if a == 0:
                 empty_s(s_win, 0, a, b)
                 empty_s(s_own, 0, a, b)
             else:
                 nc.vector.tensor_scalar(s_win[0][:, a:b], bank[:, a:b], -0.0625, None, ALU.mult)
         for t in range(1, PACK):
-            product(s_ps[t], t, d_codes[t], d_plane, x_codes, x_plane, 0, S)
+            for a, b in halves:
+                product(s_ps[t], t, d_codes[t], d_plane, x_codes[a // HALF][:], x_plane, a, b)
             empty_s(s_win, t, 0, S)
             empty_s(s_own, t, 0, HALF)
         for t in range(PACK):
@@ -151,15 +155,19 @@ def tile_picked_keytrimnorm2_none_p_kernel(tc, x_words, x_scales, d_words, d_sca
 
         def step_uv(k):
             t, a, b = steps[k]
-            u[k] = ring.tile([P, b - a], F32, name="u")
+            u[k] = low[t][:, a:b] if k + 1 == len(steps) else ring.tile([P, b - a], F32, name="u")
             v[k] = ring.tile([P, b - a], F32, name="v")
             nc.vector.tensor_tensor(u[k][:], s_win[t][:].indirect(entries(n2_t, a, b)), e[k][:], ALU.subtract)
             nc.vector.tensor_tensor(v[k][:], s_win[t][:].indirect(entries(n3_t, a, b)), e[k][:], ALU.subtract)
 
         def step_z(k):
             t, a, b = steps[k]
-            nc.vector.tensor_tensor(low[t][:, a:b], u[k][:], v[k][:], ALU.min)
-            nc.scalar.activation(z_grouped[:, a:b, t], low[t][:, a:b], ACT.Copy, scale=gn_t[:, t : t + 1])
+            if k + 1 < len(steps):
+                nc.vector.tensor_tensor(low[t][:, a:b], u[k][:], v[k][:], ALU.min)
+                nc.scalar.activation(z_grouped[:, a:b, t], low[t][:, a:b], ACT.Copy, scale=gn_t[:, t : t + 1])
+            else:
+                nc.vector.tensor_tensor(low[t - 1][:, a:b], u[k][:], v[k][:], ALU.min)
+                nc.vector.tensor_scalar(z_grouped[:, a:b, t], low[t - 1][:, a:b], gn_t[:, t : t + 1], None, ALU.mult)
 
         def h_bank(t, a, b):
             early = b <= HALF or (t, b) == (0, HALF + P)
@@ -169,7 +177,7 @@ def tile_picked_keytrimnorm2_none_p_kernel(tc, x_words, x_scales, d_words, d_sca
             nc.vector.quantize_mx(out=z_codes[:, a:b].bitcast(FP8X4), scales=z_plane[:, a:b],
                                   in_=z_grouped[:, a:b, :].rearrange("p c t -> p (c t)"))
             for t in range(PACK):
-                product(h_bank(t, a, b), t, w_codes[:, t * P : (t + 1) * P], w_plane, z_codes, z_plane, a, b)
+                product(h_bank(t, a, b), t, w_codes[:, t * P : (t + 1) * P], w_plane, z_codes[:, a:b], z_plane, a, b)
 
         def empty_abs(dst, t, a, b):
             nc.scalar.activation(dst[t][:, a:b], h_bank(t, a, b)[:, a:b], ACT.Abs)
@@ -193,10 +201,11 @@ def tile_picked_keytrimnorm2_none_p_kernel(tc, x_words, x_scales, d_words, d_sca
             if k == PACK:
                 nc.vector.quantize_mx(out=w_codes[:].bitcast(FP8X4), scales=w_plane[:], in_=w_grouped[:])
                 second(0, HALF)
+            if k + 1 == len(steps):
+                second(HALF, HALF + P)
             step_z(k)
             if PACK <= k < 2 * PACK:
                 first_half_out(k - PACK)
-        second(HALF, HALF + P)
         second(HALF + P, S)
 
         den = [keep.tile([P, S], F32, name=f"den{t}") for t in range(PACK)]
@@ -205,11 +214,12 @@ def tile_picked_keytrimnorm2_none_p_kernel(tc, x_words, x_scales, d_words, d_sca
         res = [keep.tile([P, S], F32, name=f"res{t}") for t in range(PACK)]
         out_rows = out.rearrange("(p t) j -> p t j", t=PACK)
 
-        def step_den(t, pieces):
+        def step_den(t, pieces, cuts):
             for a, b in pieces:
                 empty_abs(a_win, t, a, b)
                 empty_abs(a_own, t, a, b)
-            nc.vector.tensor_tensor(den[t][:], a_win[t][:].indirect(n5_t[:]), a_own[t][:], ALU.add)
+            for a, b in cuts:
+                nc.vector.tensor_tensor(den[t][:, a:b], a_win[t][:].indirect(entries(n5_t, a, b)), a_own[t][:, a:b], ALU.add)
 
         def step_out(t, pieces):
             nc.scalar.activation(root[t][:], den[t][:], ACT.Abs_reciprocal_sqrt, bias=0.5)
@@ -221,11 +231,11 @@ def tile_picked_keytrimnorm2_none_p_kernel(tc, x_words, x_scales, d_words, d_sca
                 nc.sync.dma_start(out_rows[:, t, a:b], res[t][:, a:b])
 
         steps_b = [(HALF, HALF + P), (HALF + P, S)]
-        step_den(0, steps_b)
-        step_den(1, halves[1:])
-        step_den(2, halves[1:])
+        step_den(0, steps_b, halves)
+        step_den(1, halves[1:], [(0, S)])
+        step_den(2, halves[1:], [(0, S)])
         step_out(0, [(0, S)])
-        step_den(3, halves[1:])
+        step_den(3, halves[1:], [(0, S)])
         step_out(1, [(0, S)])
         step_out(2, [(0, S)])
         step_out(3, [(0, S - P), (S - P, S)])

from contextlib import ExitStack

import concourse.mybir as mybir

K, T, S, N, G, H = 512, 2048, 512, 512, 2048, 512
FLOPS = 2 * K * H * S + 2 * H * N * S

F32 = mybir.dt.float32
BF16 = mybir.dt.bfloat16
I32 = mybir.dt.int32
U32 = mybir.dt.uint32
U16 = mybir.dt.uint16
U8 = mybir.dt.uint8
FP8X4 = mybir.dt.float8_e4m3fn_x4
ALU = mybir.AluOpType
ACT = mybir.ActivationFunctionType

P = 128
PACK = 4
STRIPE = 16
X_ZERO_SPLIT = 768
D_EARLY = 512


def tile_picked_keytrimnorm2_none_p_kernel(tc, x_words, x_scales, d_words, d_scales, gn, w1, offs, kidx, n1, n2, n3, n4, n5, out):
    nc = tc.nc
    with ExitStack() as ctx:
        keep = ctx.enter_context(tc.tile_pool(name="keep", bufs=1))
        ring = ctx.enter_context(tc.tile_pool(name="ring", bufs=2))
        psum = ctx.enter_context(tc.psum_pool(name="psum", bufs=1))

        def load_list(src, name):
            t = keep.tile([P, S // STRIPE], U16, name=name)
            nc.sync.dma_start(t[:], src)
            return t

        def entries(lst, a, b):
            return lst[:, a // STRIPE : b // STRIPE]

        last = PACK - 1
        HALF = S // 2
        halves = [(0, HALF), (HALF, S)]

        d_byte_table = keep.tile([P, G], U8, name="d_byte_table")
        x_byte_table = keep.tile([P, T], U8, name="x_byte_table", tag="picked")
        nc.vector.memset(d_byte_table[:].bitcast(I32), 0)
        nc.vector.memset(x_byte_table[:, :X_ZERO_SPLIT].bitcast(I32), 0)
        nc.gpsimd.memset(x_byte_table[:, X_ZERO_SPLIT:].bitcast(I32), 0)
        planes = keep.tile([P, H + S], U8, name="planes", align_bytes=64)
        nc.gpsimd.memset(planes[:].bitcast(I32), 0)

        d_word_table = keep.tile([P, G], U32, name="d_word_table")
        d_word_rows = d_words[0].rearrange("p c r -> p (c r)").bitcast(I32)
        x_word_table = keep.tile([P, T], U32, name="x_word_table", tag="table")
        kidx_t = load_list(kidx, "kidx_t")
        nc.sync.dma_start(d_word_table[:, :D_EARLY].bitcast(I32), d_word_rows[:, :D_EARLY])
        offs_t = load_list(offs, "offs_t")
        nc.sync.dma_start(d_byte_table[0:P:8, :].bitcast(I32), d_scales[0].bitcast(I32))
        n1_t = load_list(n1, "n1_t")
        n2_t = load_list(n2, "n2_t")
        nc.sync.dma_start(x_byte_table[0:P:8, :].bitcast(I32), x_scales[0].bitcast(I32))
        nc.sync.dma_start(d_word_table[:, D_EARLY:].bitcast(I32), d_word_rows[:, D_EARLY:])
        nc.sync.dma_start(x_word_table[:].bitcast(I32), x_words[0].rearrange("p c r -> p (c r)").bitcast(I32))
        n3_t = load_list(n3, "n3_t")
        n5_t = load_list(n5, "n5_t")
        n4_t = load_list(n4, "n4_t")

        warm = keep.tile([P, 2], F32, name="warm")
        nc.vector.memset(warm[:, 0:1], 1.0)
        nc.scalar.activation(warm[:, 1:2], warm[:, 0:1], ACT.Abs_reciprocal_sqrt)

        d_bytes = keep.tile([P, H], U8, name="d_bytes")
        nc.vector.tensor_copy(d_bytes[:], d_byte_table[:].indirect(kidx_t[:]))
        x_bytes = keep.tile([P, S], U8, name="x_bytes")
        nc.vector.tensor_copy(x_bytes[:], x_byte_table[:].indirect(offs_t[:]))
        spread = keep.tile([P, H + S], U8, name="spread")
        nc.vector.tensor_copy(spread[:, :H].rearrange("p (t m) -> p t m", t=PACK), d_bytes[:].rearrange("p (m t) -> p t m", t=PACK))
        nc.vector.tensor_copy(spread[:, H:].bitcast(I32), x_bytes[:].bitcast(I32))
        for q in range(4):
            (nc.scalar, nc.sync)[q % 2].dma_start(planes[32 * q : 32 * q + 4, :].bitcast(I32), spread[32 * q : 32 * q + 32 : 8, :].bitcast(I32))
        d_plane = planes[:, :H]
        x_plane = planes[:, H:]
        d_picked = keep.tile([P, H], U32, name="d_picked", tag="picked")
        nc.vector.tensor_copy(d_picked[:], d_word_table[:].indirect(kidx_t[:]))
        x_codes = [keep.tile([P, HALF], U32, name=f"x_codes{i}", align_bytes=64) for i in range(2)]
        nc.vector.tensor_copy(x_codes[0][:], x_word_table[:].indirect(entries(offs_t, 0, HALF)))
        d_first = keep.tile([P, P], U32, name="d_first", align_bytes=64)
        d_rest = keep.tile([P, PACK - 1, P], U32, name="d_rest", align_bytes=64)
        d_codes = [d_first[:]] + [d_rest[:, t, :] for t in range(PACK - 1)]
        picked = d_picked[:].rearrange("p (m t) -> p m t", t=PACK)
        nc.vector.tensor_copy(d_first[:], picked[:, :, 0])
        nc.vector.tensor_copy(x_codes[1][:], x_word_table[:].indirect(entries(offs_t, HALF, S)))
        nc.vector.tensor_copy(d_rest[:].rearrange("p t m -> p m t"), picked[:, :, 1:])

        w_raw = keep.tile([P, PACK, N], F32, name="w_raw", tag="table")
        nc.sync.dma_start(w_raw[:], w1.rearrange("(p j) m -> p j m", j=PACK))

        gn_t = keep.tile([P, PACK], F32, name="gn_t", tag="picked")
        nc.sync.dma_start(gn_t[:], gn.rearrange("(p t) o -> p (t o)", t=PACK))

        s_ps = [psum.tile([P, S], F32, name=f"s_ps{t}") for t in range(PACK)]
        h_ps = [psum.tile([P, S], F32, name=f"h_ps{t}") for t in range(PACK)]
        s_win = [keep.tile([P, S], F32, name=f"s_win{t}") for t in range(PACK)]
        h_win = [keep.tile([P, 2 * S], F32, name=f"h_win{t}") for t in range(PACK)]
        a_win = [keep.tile([P, 2 * S], F32, name=f"a_win{t}") for t in range(PACK)]
        s_own = [h_win[t][:, S:] for t in range(PACK)]
        low = [a_win[t][:, S:] for t in range(PACK)]
        a_own = [keep.tile([P, S], F32, name=f"a_own{t}") for t in range(PACK)]

        def product(bank, t, lhs, lhs_plane, rhs, rhs_plane, a, b):
            cols = slice(t * P, (t + 1) * P)
            nc.tensor.matmul_mx(out=bank[:, a:b], lhsT=lhs.bitcast(FP8X4), lhsT_scale=lhs_plane[:, cols],
                                rhs=rhs.bitcast(FP8X4), rhs_scale=rhs_plane[:, a:b], start=True, stop=True)

        def empty_s(dst, t, a, b):
            bank = h_ps[0] if (t, b) == (0, HALF) else s_ps[t]
            nc.scalar.activation(dst[t][:, a:b], bank[:, a:b], ACT.Copy, scale=-0.0625)

        for bank, (a, b) in zip((h_ps[0], s_ps[0]), halves):
            product(bank, 0, d_codes[0], d_plane, x_codes[a // HALF][:], x_plane, a, b)
            if a == 0:
                empty_s(s_win, 0, a, b)
                empty_s(s_own, 0, a, b)
            else:
                nc.vector.tensor_scalar(s_win[0][:, a:b], bank[:, a:b], -0.0625, None, ALU.mult)
        for t in range(1, PACK):
            for a, b in halves:
                product(s_ps[t], t, d_codes[t], d_plane, x_codes[a // HALF][:], x_plane, a, b)
            empty_s(s_win, t, 0, S)
            empty_s(s_own, t, 0, HALF)
        for t in range(PACK):
            nc.sync.dma_start(s_own[t][:, HALF:], s_win[t][:, HALF:])

        w_grouped = keep.tile([P, N * PACK], BF16, name="w_grouped", align_bytes=64)
        w_codes = keep.tile([P, N], U32, name="w_codes", align_bytes=64)
        w_plane = keep.tile([P, N], U8, name="w_plane", align_bytes=64)

        def cast_w(part):
            ms = slice(part * P // PACK, (part + 1) * P // PACK)
            nc.scalar.copy(w_grouped[:].rearrange("p (t m j) -> p m t j", t=PACK, j=PACK)[:, ms],
                           w_raw[:].rearrange("p j (m t) -> p m t j", t=PACK)[:, ms])

        z_grouped = keep.tile([P, S, PACK], BF16, name="z_grouped", align_bytes=64)
        z_codes = keep.tile([P, S], U32, name="z_codes", align_bytes=64)
        z_plane = keep.tile([P, S], U8, name="z_plane", align_bytes=64)

        steps = [(t, a, b) for a, b in halves for t in range(PACK)]
        steps[-1:] = [(last, HALF, HALF + P), (last, HALF + P, S)]
        e, u, v = {}, {}, {}

        def step_e(k):
            t, a, b = steps[k]
            e[k] = ring.tile([P, b - a], F32, name="e", bufs=3)
            nc.vector.tensor_tensor(e[k][:], s_win[t][:].indirect(entries(n1_t, a, b)), s_own[t][:, a:b], ALU.add)

        def step_uv(k):
            t, a, b = steps[k]
            u[k] = low[t][:, a:b] if k + 1 == len(steps) else ring.tile([P, b - a], F32, name="u")
            v[k] = ring.tile([P, b - a], F32, name="v")
            nc.vector.tensor_tensor(u[k][:], s_win[t][:].indirect(entries(n2_t, a, b)), e[k][:], ALU.subtract)
            nc.vector.tensor_tensor(v[k][:], s_win[t][:].indirect(entries(n3_t, a, b)), e[k][:], ALU.subtract)

        def step_z(k):
            t, a, b = steps[k]
            if k + 1 < len(steps):
                nc.vector.tensor_tensor(low[t][:, a:b], u[k][:], v[k][:], ALU.min)
                nc.scalar.activation(z_grouped[:, a:b, t], low[t][:, a:b], ACT.Copy, scale=gn_t[:, t : t + 1])
            else:
                nc.vector.tensor_tensor(low[t - 1][:, a:b], u[k][:], v[k][:], ALU.min)
                nc.vector.tensor_scalar(z_grouped[:, a:b, t], low[t - 1][:, a:b], gn_t[:, t : t + 1], None, ALU.mult)

        def h_bank(t, a, b):
            early = b <= HALF or (t, b) == (0, HALF + P)
            return (h_ps if early else s_ps)[t]

        def second(a, b):
            nc.vector.quantize_mx(out=z_codes[:, a:b].bitcast(FP8X4), scales=z_plane[:, a:b],
                                  in_=z_grouped[:, a:b, :].rearrange("p c t -> p (c t)"))
            for t in range(PACK):
                product(h_bank(t, a, b), t, w_codes[:, t * P : (t + 1) * P], w_plane, z_codes[:, a:b], z_plane, a, b)

        def empty_abs(dst, t, a, b):
            nc.scalar.activation(dst[t][:, a:b], h_bank(t, a, b)[:, a:b], ACT.Abs)

        def empty_h(t, a, b):
            nc.scalar.copy(h_win[t][:, a:b], h_bank(t, a, b)[:, a:b])

        def first_half_out(t):
            empty_abs(a_win, t, 0, HALF)
            nc.sync.dma_start(a_own[t][:, :HALF], a_win[t][:, :HALF])
            empty_h(t, 0, HALF)

        step_e(0)
        step_e(1)
        for k in range(len(steps)):
            step_uv(k)
            if k + 2 < len(steps):
                step_e(k + 2)
            if k < PACK:
                cast_w(k)
            if k == PACK:
                nc.vector.quantize_mx(out=w_codes[:].bitcast(FP8X4), scales=w_plane[:], in_=w_grouped[:])
                second(0, HALF)
            if k + 1 == len(steps):
                second(HALF, HALF + P)
            step_z(k)
            if PACK <= k < 2 * PACK:
                first_half_out(k - PACK)
        second(HALF + P, S)

        den = [keep.tile([P, S], F32, name=f"den{t}") for t in range(PACK)]
        root = [keep.tile([P, S], F32, name=f"root{t}") for t in range(PACK)]
        inv = [keep.tile([P, S], F32, name=f"inv{t}") for t in range(PACK)]
        res = [keep.tile([P, S], F32, name=f"res{t}") for t in range(PACK)]
        out_rows = out.rearrange("(p t) j -> p t j", t=PACK)

        def step_den(t, pieces, cuts):
            for a, b in pieces:
                empty_abs(a_win, t, a, b)
                empty_abs(a_own, t, a, b)
            for a, b in cuts:
                nc.vector.tensor_tensor(den[t][:, a:b], a_win[t][:].indirect(entries(n5_t, a, b)), a_own[t][:, a:b], ALU.add)

        def step_out(t, pieces):
            nc.scalar.activation(root[t][:], den[t][:], ACT.Abs_reciprocal_sqrt, bias=0.5)
            nc.scalar.activation(inv[t][:], root[t][:], ACT.Square)
            for a, b in steps_b if t == 0 else halves[1:]:
                empty_h(t, a, b)
            for a, b in pieces:
                nc.vector.tensor_tensor(res[t][:, a:b], h_win[t][:].indirect(entries(n4_t, a, b)), inv[t][:, a:b], ALU.mult)
                nc.sync.dma_start(out_rows[:, t, a:b], res[t][:, a:b])

        steps_b = [(HALF, HALF + P), (HALF + P, S)]
        step_den(0, steps_b, halves)
        step_den(1, halves[1:], [(0, S)])
        step_den(2, halves[1:], [(0, S)])
        step_out(0, [(0, S)])
        step_den(3, halves[1:], [(0, S)])
        step_out(1, [(0, S)])
        step_out(2, [(0, S)])
        step_out(3, [(0, S - P), (S - P, S)])
